import numpy as np
import ml_dtypes


def mxq(x, axis, fmt="e4m3"):
    dtype, down = {"e4m3": (ml_dtypes.float8_e4m3fn, 7), "e5m2": (ml_dtypes.float8_e5m2, 14)}[fmt]
    v = np.moveaxis(np.asarray(x, np.float32).astype(ml_dtypes.bfloat16).astype(np.float64), axis, -1)
    blocks = v.reshape(v.shape[:-1] + (-1, 32))
    amax = np.abs(blocks).max(-1, keepdims=True)
    byte = np.maximum(np.where(amax > 0, np.frexp(amax)[1] - 1 + 127, 0) - down, 1)
    scale = np.exp2(byte - 127.0)
    codes = (blocks / scale).astype(np.float32).astype(dtype).astype(np.float64)
    return np.moveaxis((codes * scale).reshape(v.shape), -1, axis)


WIDE = False


def mx_kscale(k):
    if not WIDE:
        return np.ones(k)
    levels = np.array([10, -10, 5, -5, 0])
    if k % 512:
        return np.exp2(np.random.permutation(np.resize(levels, k // 32))).repeat(32)
    a = np.empty((k // 512, 16))
    for p in range(k // 512):
        a[p, :8] = np.random.permutation(np.resize(levels, 8))
        for g in range(8):
            far = levels[np.abs(levels - a[p, g]) >= 10]
            a[p, g + 8] = far[np.random.randint(len(far))]
    return np.exp2(a.ravel()).repeat(32)


def f64(x):
    return np.asarray(x).astype(np.float64)


def striped(idx):
    return np.tile(idx.reshape(-1, 16).T, (8, 1)).astype(np.uint16)


def unstriped(offs):
    return offs[:16].T.reshape(-1).astype(np.int64)


def striped8(idx):
    return np.concatenate([x.reshape(-1, 16).T for x in idx]).astype(np.uint16)


def runs(offs, k):
    lists = np.stack([offs[16 * r : 16 * r + 16].T.reshape(-1) for r in range(8)]).astype(np.int64)
    return lists[np.arange(k) % 512 // 64]


def pack_weight(w):
    k, n = w.shape
    w = f64(np.asarray(w, np.float32).astype(ml_dtypes.bfloat16)).reshape(k // 32, 32, n)
    amax = np.abs(w).max(1)
    byte = np.clip(np.where(amax > 0, np.frexp(amax)[1] - 1 + 127 - 7, 1), 1, 254)
    scaled = (w * np.exp2(127.0 - byte)[:, None, :]).reshape(k, n).astype(np.float32)
    words = np.ascontiguousarray(scaled.reshape(k // 512, 128, 4, n).transpose(0, 1, 3, 2)).astype(ml_dtypes.float8_e4m3fn).view(np.uint8)
    return words, np.ascontiguousarray(byte.astype(np.uint8).reshape(k // 512, 16, n))


def unpack_weight(words, scales):
    g, p, n, _ = words.shape
    vals = np.ascontiguousarray(words).view(ml_dtypes.float8_e4m3fn).astype(np.float64) * np.repeat(np.exp2(scales.astype(np.float64) - 127.0), 8, axis=1)[..., None]
    return vals.transpose(0, 1, 3, 2).reshape(g * 512, n)


def sigmoid(v):
    return 1.0 / (1.0 + np.exp(-np.maximum(v, -700.0)))

def planes(y):
    n, m = y.shape
    v = y.astype(np.float32).astype(ml_dtypes.bfloat16).astype(np.float64).reshape(n // 32, 32, m)
    top = np.abs(v).max(1)
    byte = np.clip(np.where(top > 0, np.frexp(top)[1] - 1 + 127 - 7, 1), 1, 254)
    codes = (v * np.exp2(127.0 - byte)[:, None, :]).reshape(n, m).astype(np.float32).astype(ml_dtypes.float8_e4m3fn).view(np.uint8)
    words = codes.reshape(n // 512, 128, 4, m).transpose(0, 1, 3, 2)
    return np.ascontiguousarray(words), np.ascontiguousarray(byte.astype(np.uint8).reshape(n // 512, 16, m))


K, T, S, N, H = 512, 2048, 512, 512, 512


def setup_inputs():
    n = np.random.standard_normal
    s = mx_kscale(K)[:, None]
    u = mx_kscale(H)
    packed_xT = pack_weight(n((K, T)) * s)
    packed_w1 = pack_weight(n((K, H)) / np.sqrt(K) / s)
    packed_w2 = pack_weight(n((H, N)) / np.sqrt(H) / u[:, None])
    packed_w3 = pack_weight(n((H, N)) / np.sqrt(H) / u[:, None])
    return {
        "x_words": packed_xT[0],
        "x_scales": packed_xT[1],
        "w1_words": packed_w1[0],
        "w1_scales": packed_w1[1],
        "gn": (np.random.uniform(0.5, 1.5, (H, 1)) * u[:, None]).astype(np.float32),
        "w2_words": packed_w2[0],
        "w2_scales": packed_w2[1],
        "gm": (np.random.uniform(0.5, 1.5, (H, 1)) * u[:, None]).astype(np.float32),
        "w3_words": packed_w3[0],
        "w3_scales": packed_w3[1],
        "offs": striped(np.random.permutation(T)[:S]),
        "n1": striped8(np.stack([np.random.permutation(S) for _ in range(8)])),
        "n2": striped8(np.stack([np.random.permutation(S) for _ in range(8)])),
        "n3": striped8(np.stack([np.random.permutation(S) for _ in range(8)])),
        "n4": striped8(np.stack([np.random.permutation(S) for _ in range(8)])),
        "n5": striped8(np.stack([np.random.permutation(S) for _ in range(8)])),
        "n6": striped8(np.stack([np.random.permutation(S) for _ in range(8)])),
        "n7": striped8(np.stack([np.random.permutation(S) for _ in range(8)])),
    }


def reference(x_words, x_scales, w1_words, w1_scales, gn, w2_words, w2_scales, gm, w3_words, w3_scales, offs, n1, n2, n3, n4, n5, n6, n7):
    xq = unpack_weight(x_words, x_scales)[:, unstriped(offs)]
    y = unpack_weight(w1_words, w1_scales).T @ xq
    z = f64(gn) * ((y * (y[np.arange(H)[:, None], runs(n1, H)])) * (np.tanh(y[np.arange(H)[:, None], runs(n2, H)])))
    a = unpack_weight(w2_words, w2_scales).T @ mxq(z, 0, "e4m3")
    st = y[np.arange(H)[:, None], runs(n3, H)] - y
    z2 = f64(gm) * (y * (sigmoid(st[np.arange(H)[:, None], runs(n4, H)])))
    b = unpack_weight(w3_words, w3_scales).T @ mxq(z2, 0, "e4m3")
    out_0 = np.maximum(np.minimum(a - (0.5 * (a[np.arange(N)[:, None], runs(n5, N)])), b[np.arange(N)[:, None], runs(n6, N)]), b[np.arange(N)[:, None], runs(n7, N)])
    return (out_0,) + planes(out_0)

@@ -1,0 +1,231 @@
+from contextlib import ExitStack
+
+import concourse.mybir as mybir
+
+K, T, S, N, H = 512, 2048, 512, 512, 512
+FLOPS = 2 * K * H * S + 2 * 2 * H * N * S
+
+F32 = mybir.dt.float32
+BF16 = mybir.dt.bfloat16
+I32 = mybir.dt.int32
+U32 = mybir.dt.uint32
+U16 = mybir.dt.uint16
+U8 = mybir.dt.uint8
+FP8X4 = mybir.dt.float8_e4m3fn_x4
+ALU = mybir.AluOpType
+ACT = mybir.ActivationFunctionType
+
+P = 128
+PACK = 4
+HALF = S // 2
+QUARTER = S // 4
+LANES = 16
+
+
+def tile_picked_forkclampbcubehopd_none_po_kernel(tc, x_words, x_scales, w1_words, w1_scales, gn, w2_words, w2_scales, gm, w3_words, w3_scales, offs, n1, n2, n3, n4, n5, n6, n7, out_0, out_1, out_2):
+    nc = tc.nc
+
+    def words_in_hbm(words):
+        return words[0].rearrange("p c r -> p (c r)").bitcast(I32)
+
+    def load_scale_rows(queue, plane, first_row, scales, quadrants=range(4)):
+        for q in quadrants:
+            row = 32 * q + first_row
+            queue.dma_start(out=plane[row : row + 4, :].bitcast(I32), in_=scales[0, 4 * q : 4 * q + 4, :].bitcast(I32))
+
+    def deal_columns(dealt, raw):
+        nc.vector.tensor_copy(
+            out=dealt.rearrange("p (t c i) -> p c t i", t=PACK, i=4),
+            in_=raw.rearrange("p (c i t) -> p c t i", t=PACK, i=4),
+        )
+
+    def cols(h, width=HALF):
+        return slice(h * width, (h + 1) * width)
+
+    def looked_up(window, places, h, width=HALF):
+        return window[:].indirect(places[:, h * width // LANES : (h + 1) * width // LANES])
+
+    def by_fours(planes):
+        return planes.rearrange("p t (c i) -> p c t i", i=4)
+
+    def woven(tile):
+        return tile.rearrange("p (c i t) -> p c t i", i=4, t=PACK)
+
+    with ExitStack() as ctx:
+        keep = ctx.enter_context(tc.tile_pool(name="keep", bufs=1))
+        psum = ctx.enter_context(tc.psum_pool(name="psum", bufs=1))
+
+        def load_list(name, places):
+            tile = keep.tile([P, S // LANES], U16, name=name)
+            nc.sync.dma_start(tile[:], places)
+            return tile
+
+        def planes_tile(name):
+            return [keep.tile([P, S], F32, name=f"{name}{t}") for t in range(PACK)]
+
+        x_plane = keep.tile([P, T], U8)
+        nc.vector.memset(x_plane[:].bitcast(I32), 0)
+        w1_plane = keep.tile([P, H], U8)
+        nc.gpsimd.memset(w1_plane[:].bitcast(I32), 0)
+        w23_plane = keep.tile([P, N], U8)
+        nc.vector.memset(w23_plane[:].bitcast(I32), 0)
+        warm = keep.tile([P, 2], F32)
+        nc.vector.memset(warm[:, 0:1], 0.0)
+        nc.scalar.activation(warm[:, 1:2], warm[:, 0:1], ACT.Sigmoid)
+
+        y = [keep.tile([P, 2 * S], F32, name=f"y{t}") for t in range(PACK)]
+        for t in range(PACK):
+            nc.vector.memset(y[t][:, S:], 0.0)
+
+        offs_sb = load_list("offs_sb", offs)
+        n3_sb = load_list("n3_sb", n3)
+        x_codes = keep.tile([P, T], I32)
+        nc.sync.dma_start(out=x_codes[:], in_=words_in_hbm(x_words))
+        load_scale_rows(nc.sync, x_plane, 0, x_scales)
+        w1_raw = keep.tile([P, H], I32)
+        nc.sync.dma_start(out=w1_raw[:], in_=words_in_hbm(w1_words))
+        load_scale_rows(nc.sync, w1_plane, 0, w1_scales, range(0, 2))
+        load_scale_rows(nc.gpsimd, w1_plane, 0, w1_scales, range(2, 4))
+        w3_raw = keep.tile([P, N], I32)
+        nc.sync.dma_start(out=w3_raw[:], in_=words_in_hbm(w3_words))
+        w2_raw = keep.tile([P, N], I32)
+        nc.sync.dma_start(out=w2_raw[:], in_=words_in_hbm(w2_words))
+        gm_sb = keep.tile([P, PACK], F32)
+        nc.sync.dma_start(out=gm_sb[:], in_=gm.rearrange("(p t) o -> p (t o)", t=PACK))
+        n4_sb = load_list("n4_sb", n4)
+        n1_sb = load_list("n1_sb", n1)
+        n2_sb = load_list("n2_sb", n2)
+        gn_sb = keep.tile([P, PACK], F32)
+        nc.sync.dma_start(out=gn_sb[:], in_=gn.rearrange("(p t) o -> p (t o)", t=PACK))
+        load_scale_rows(nc.sync, w23_plane, 4, w3_scales)
+        load_scale_rows(nc.sync, w23_plane, 0, w2_scales)
+        n6_sb = load_list("n6_sb", n6)
+        n7_sb = load_list("n7_sb", n7)
+        n5_sb = load_list("n5_sb", n5)
+
+        w1_codes = keep.tile([P, H], I32, align_bytes=64)
+        deal_columns(w1_codes[:], w1_raw[:])
+        w1_dealt = keep.tile([P, H], U8, align_bytes=64)
+        deal_columns(w1_dealt[:], w1_plane[:])
+        xq_scales = keep.tile([P, S], U8, align_bytes=64)
+        nc.vector.tensor_copy(xq_scales[:], x_plane[:].indirect(offs_sb[:]))
+        xq_codes = keep.tile([P, S], U32, align_bytes=64)
+        for h in range(2):
+            nc.vector.tensor_copy(xq_codes[:, cols(h)], x_codes[:].bitcast(U32).indirect(offs_sb[:, h * HALF // LANES : (h + 1) * HALF // LANES]))
+
+        def product(name, w_codes, w_scales, codes, scales):
+            banks = [psum.tile([P, S], F32, name=f"{name}{t}") for t in range(PACK)]
+            for h in range(2):
+                for t in range(PACK):
+                    nc.tensor.matmul_mx(
+                        out=banks[t][:, cols(h)],
+                        lhsT=w_codes[:, cols(t, P)].bitcast(FP8X4),
+                        lhsT_scale=w_scales[:, cols(t, P)],
+                        rhs=codes[:, cols(h)].bitcast(FP8X4),
+                        rhs_scale=scales[:, cols(h)],
+                        start=True,
+                        stop=True,
+                    )
+            return banks
+
+        y_banks = product("ab", w1_codes, w1_dealt[:], xq_codes, xq_scales)
+        b = [keep.tile([P, 2 * S], F32, name=f"b_sb{t}") for t in range(PACK)]
+        y_plain = [b[t][:, S:] for t in range(PACK)]
+        for t in range(PACK):
+            nc.scalar.copy(y[t][:, :S], y_banks[t][:])
+            nc.scalar.copy(y_plain[t], y_banks[t][:])
+
+        st = planes_tile("st")
+        for t in range(PACK):
+            nc.vector.tensor_tensor(st[t][:], y[t][:].indirect(n3_sb[:]), y_plain[t], ALU.subtract)
+        gained = keep.tile([P, PACK, S], F32)
+        for t in range(PACK):
+            nc.vector.tensor_scalar(gained[:, t, :], y_plain[t], gm_sb[:, t : t + 1], None, ALU.mult)
+        gate = [keep.tile([P, PACK, HALF], F32, name=f"gate{h}") for h in range(2)]
+        for h in range(2):
+            for t in range(PACK):
+                nc.scalar.activation(gate[h][:, t, :], looked_up(st[t], n4_sb, h), ACT.Sigmoid)
+        z2_bf = keep.tile([P, PACK * S], BF16, tag="held_a", align_bytes=64)
+        z2_codes = keep.tile([P, S], U32, align_bytes=64)
+        z2_scales = keep.tile([P, S], U8, align_bytes=64)
+        for h in range(2):
+            nc.vector.tensor_tensor(woven(z2_bf[:, cols(h, PACK * HALF)]), by_fours(gate[h][:]), by_fours(gained[:, :, cols(h)]), ALU.mult)
+        for h in range(2):
+            nc.vector.quantize_mx(out=z2_codes[:, cols(h)].bitcast(FP8X4), scales=z2_scales[:, cols(h)], in_=z2_bf[:, cols(h, PACK * HALF)])
+        w3_codes = keep.tile([P, N], I32, align_bytes=64)
+        deal_columns(w3_codes[:], w3_raw[:])
+        w23_dealt = keep.tile([P, N], U8, align_bytes=64)
+        deal_columns(w23_dealt[:], w23_plane[:])
+        b_banks = product("b", w3_codes, w23_dealt[4:, :], z2_codes, z2_scales)
+        for t in range(PACK):
+            nc.scalar.copy(b[t][:, :S], b_banks[t][:])
+
+        pair = [keep.tile([P, PACK, HALF], F32, name="pair0"), keep.tile([P, PACK, HALF], F32, name="pair1", tag="held_a", align_bytes=64)]
+        for h in range(2):
+            for t in range(PACK):
+                nc.vector.tensor_tensor(pair[h][:, t, :], looked_up(y[t], n1_sb, h), y_plain[t][:, cols(h)], ALU.mult)
+        gn_twice = keep.tile([P, PACK], F32)
+        gn_minus = keep.tile([P, PACK], F32)
+        nc.vector.tensor_scalar(gn_twice[:], gn_sb[:], 2.0, 0.0, ALU.mult, ALU.add)
+        nc.vector.tensor_scalar(gn_minus[:], gn_sb[:], -1.0, 0.0, ALU.mult, ALU.add)
+        sig = [keep.tile([P, PACK, HALF], F32, name=f"sig{h}") for h in range(2)]
+        bent = [keep.tile([P, PACK, HALF], F32, name=f"bent{h}") for h in range(2)]
+        for h in range(2):
+            for t in range(PACK):
+                nc.scalar.activation(sig[h][:, t, :], looked_up(y[t], n2_sb, h), ACT.Sigmoid, scale=2.0)
+            for t in range(PACK):
+                nc.scalar.activation(bent[h][:, t, :], sig[h][:, t, :], ACT.Identity, scale=gn_twice[:, t : t + 1], bias=gn_minus[:, t : t + 1])
+        z_bf = keep.tile([P, PACK * S], BF16, tag="held_b", align_bytes=64)
+        z_codes = keep.tile([P, S], U32, align_bytes=64)
+        z_scales = keep.tile([P, S], U8, align_bytes=64)
+        for h in range(2):
+            nc.vector.tensor_tensor(woven(z_bf[:, cols(h, PACK * HALF)]), by_fours(pair[h][:]), by_fours(bent[h][:]), ALU.mult)
+        for h in range(2):
+            nc.vector.quantize_mx(out=z_codes[:, cols(h)].bitcast(FP8X4), scales=z_scales[:, cols(h)], in_=z_bf[:, cols(h, PACK * HALF)])
+        w2_codes = keep.tile([P, N], I32, align_bytes=64)
+        deal_columns(w2_codes[:], w2_raw[:])
+        a_banks = product("ab", w2_codes, w23_dealt[:], z_codes, z_scales)
+        a_half = planes_tile("a_half")
+        a_plain = planes_tile("a_plain")
+        for t in range(PACK):
+            nc.scalar.activation(a_half[t][:], a_banks[t][:], ACT.Copy, scale=-0.5)
+            nc.scalar.copy(a_plain[t][:], a_banks[t][:])
+
+        ceiling = keep.tile([P, PACK, S], F32)
+        for t in range(PACK):
+            nc.vector.tensor_copy(ceiling[:, t, :], b[t][:].indirect(n6_sb[:]))
+        floor = [keep.tile([P, PACK, HALF], F32, name="floor0"), keep.tile([P, PACK, HALF], F32, name="floor1", tag="held_b", align_bytes=64)]
+        for h in range(2):
+            for t in range(PACK):
+                nc.vector.tensor_copy(floor[h][:, t, :], looked_up(b[t], n7_sb, h))
+
+        out_codes = keep.tile([P, S], U32, align_bytes=64)
+        out_scales = keep.tile([P, S], U8, align_bytes=64)
+        out_rows = out_0.rearrange("(p t) j -> p t j", t=PACK)
+        out_words = words_in_hbm(out_1)
+        pieces = [(0, 0, HALF), (1, 0, QUARTER), (1, QUARTER, QUARTER)]
+        less = [keep.tile([P, PACK, HALF], F32, name=f"less{h}") for h in range(2)]
+        for h in range(2):
+            for t in range(PACK):
+                nc.vector.tensor_tensor(less[h][:, t, :], looked_up(a_half[t], n5_sb, h), a_plain[t][:, cols(h)], ALU.add)
+            for h2, start, width in pieces:
+                if h2 != h:
+                    continue
+                inside = slice(start, start + width)
+                first = h * HALF + start
+                columns = slice(first, first + width)
+                capped = keep.tile([P, PACK, width], F32, name=f"capped{first}")
+                nc.vector.tensor_tensor(capped[:], less[h][:, :, inside], ceiling[:, :, columns], ALU.min)
+                result = keep.tile([P, PACK, width], F32, name=f"result{first}")
+                nc.vector.tensor_tensor(result[:], capped[:], floor[h][:, :, inside], ALU.max)
+                nc.sync.dma_start(out=out_rows[:, :, columns], in_=result[:])
+                result_bf = keep.tile([P, PACK * width], BF16, name=f"result_bf{first}", align_bytes=64)
+                if first + width < S:
+                    nc.scalar.copy(woven(result_bf[:]), by_fours(result[:]))
+                else:
+                    nc.vector.tensor_copy(woven(result_bf[:]), by_fours(result[:]))
+                nc.vector.quantize_mx(out=out_codes[:, columns].bitcast(FP8X4), scales=out_scales[:, columns], in_=result_bf[:])
+            nc.sync.dma_start(out=out_words[:, cols(h)], in_=out_codes[:, cols(h)].bitcast(I32))
+        for q in range(4):
+            queue = nc.scalar if q % 2 else nc.sync
+            queue.dma_start(out=out_2[0, 4 * q : 4 * q + 4, :].bitcast(I32), in_=out_scales[32 * q : 32 * q + 4, :].bitcast(I32))

@@ -20,6 +20,7 @@ PACK = 4
 HALF = S // 2
 QUARTER = S // 4
 LANES = 16
+COPIES_ON_VECTOR = 2
 
 
 def tile_picked_forkclampbcubehopd_none_po_kernel(tc, x_words, x_scales, w1_words, w1_scales, gn, w2_words, w2_scales, gm, w3_words, w3_scales, offs, n1, n2, n3, n4, n5, n6, n7, out_0, out_1, out_2):
@@ -28,8 +29,8 @@ def tile_picked_forkclampbcubehopd_none_po_kernel(tc, x_words, x_scales, w1_word
     def words_in_hbm(words):
         return words[0].rearrange("p c r -> p (c r)").bitcast(I32)
 
-    def load_scale_rows(queue, plane, first_row, scales, quadrants=range(4)):
-        for q in quadrants:
+    def load_scale_rows(queue, plane, first_row, scales):
+        for q in range(4):
             row = 32 * q + first_row
             queue.dma_start(out=plane[row : row + 4, :].bitcast(I32), in_=scales[0, 4 * q : 4 * q + 4, :].bitcast(I32))
 
@@ -64,9 +65,9 @@ def tile_picked_forkclampbcubehopd_none_po_kernel(tc, x_words, x_scales, w1_word
             return [keep.tile([P, S], F32, name=f"{name}{t}") for t in range(PACK)]
 
         x_plane = keep.tile([P, T], U8)
-        nc.vector.memset(x_plane[:].bitcast(I32), 0)
+        nc.gpsimd.memset(x_plane[:].bitcast(I32), 0)
         w1_plane = keep.tile([P, H], U8)
-        nc.gpsimd.memset(w1_plane[:].bitcast(I32), 0)
+        nc.vector.memset(w1_plane[:].bitcast(I32), 0)
         w23_plane = keep.tile([P, N], U8)
         nc.vector.memset(w23_plane[:].bitcast(I32), 0)
         warm = keep.tile([P, 2], F32)
@@ -78,18 +79,19 @@ def tile_picked_forkclampbcubehopd_none_po_kernel(tc, x_words, x_scales, w1_word
             nc.vector.memset(y[t][:, S:], 0.0)
 
         offs_sb = load_list("offs_sb", offs)
-        n3_sb = load_list("n3_sb", n3)
-        x_codes = keep.tile([P, T], I32)
-        nc.sync.dma_start(out=x_codes[:], in_=words_in_hbm(x_words))
         load_scale_rows(nc.sync, x_plane, 0, x_scales)
         w1_raw = keep.tile([P, H], I32)
         nc.sync.dma_start(out=w1_raw[:], in_=words_in_hbm(w1_words))
-        load_scale_rows(nc.sync, w1_plane, 0, w1_scales, range(0, 2))
-        load_scale_rows(nc.gpsimd, w1_plane, 0, w1_scales, range(2, 4))
+        x_codes = keep.tile([P, T], I32)
+        nc.sync.dma_start(out=x_codes[:], in_=words_in_hbm(x_words))
+        n3_sb = load_list("n3_sb", n3)
+        load_scale_rows(nc.sync, w1_plane, 0, w1_scales)
         w3_raw = keep.tile([P, N], I32)
         nc.sync.dma_start(out=w3_raw[:], in_=words_in_hbm(w3_words))
         w2_raw = keep.tile([P, N], I32)
         nc.sync.dma_start(out=w2_raw[:], in_=words_in_hbm(w2_words))
+        load_scale_rows(nc.sync, w23_plane, 4, w3_scales)
+        load_scale_rows(nc.sync, w23_plane, 0, w2_scales)
         gm_sb = keep.tile([P, PACK], F32)
         nc.sync.dma_start(out=gm_sb[:], in_=gm.rearrange("(p t) o -> p (t o)", t=PACK))
         n4_sb = load_list("n4_sb", n4)
@@ -97,26 +99,24 @@ def tile_picked_forkclampbcubehopd_none_po_kernel(tc, x_words, x_scales, w1_word
         n2_sb = load_list("n2_sb", n2)
         gn_sb = keep.tile([P, PACK], F32)
         nc.sync.dma_start(out=gn_sb[:], in_=gn.rearrange("(p t) o -> p (t o)", t=PACK))
-        load_scale_rows(nc.sync, w23_plane, 4, w3_scales)
-        load_scale_rows(nc.sync, w23_plane, 0, w2_scales)
         n6_sb = load_list("n6_sb", n6)
         n7_sb = load_list("n7_sb", n7)
         n5_sb = load_list("n5_sb", n5)
 
         w1_codes = keep.tile([P, H], I32, align_bytes=64)
         deal_columns(w1_codes[:], w1_raw[:])
-        w1_dealt = keep.tile([P, H], U8, align_bytes=64)
-        deal_columns(w1_dealt[:], w1_plane[:])
         xq_scales = keep.tile([P, S], U8, align_bytes=64)
         nc.vector.tensor_copy(xq_scales[:], x_plane[:].indirect(offs_sb[:]))
         xq_codes = keep.tile([P, S], U32, align_bytes=64)
-        for h in range(2):
-            nc.vector.tensor_copy(xq_codes[:, cols(h)], x_codes[:].bitcast(U32).indirect(offs_sb[:, h * HALF // LANES : (h + 1) * HALF // LANES]))
+        nc.vector.tensor_copy(xq_codes[:, cols(0)], x_codes[:].bitcast(U32).indirect(offs_sb[:, : HALF // LANES]))
+        w1_dealt = keep.tile([P, H], U8, align_bytes=64)
+        deal_columns(w1_dealt[:], w1_plane[:])
+        nc.vector.tensor_copy(xq_codes[:, cols(1)], x_codes[:].bitcast(U32).indirect(offs_sb[:, HALF // LANES :]))
 
         def product(name, w_codes, w_scales, codes, scales):
             banks = [psum.tile([P, S], F32, name=f"{name}{t}") for t in range(PACK)]
-            for h in range(2):
-                for t in range(PACK):
+            for t in range(PACK):
+                for h in range(2):
                     nc.tensor.matmul_mx(
                         out=banks[t][:, cols(h)],
                         lhsT=w_codes[:, cols(t, P)].bitcast(FP8X4),
@@ -133,20 +133,23 @@ def tile_picked_forkclampbcubehopd_none_po_kernel(tc, x_words, x_scales, w1_word
         y_plain = [b[t][:, S:] for t in range(PACK)]
         for t in range(PACK):
             nc.scalar.copy(y[t][:, :S], y_banks[t][:])
-            nc.scalar.copy(y_plain[t], y_banks[t][:])
+            if t < COPIES_ON_VECTOR:
+                nc.vector.tensor_copy(y_plain[t], y[t][:, :S])
+            else:
+                nc.scalar.copy(y_plain[t], y_banks[t][:])
 
         st = planes_tile("st")
         for t in range(PACK):
             nc.vector.tensor_tensor(st[t][:], y[t][:].indirect(n3_sb[:]), y_plain[t], ALU.subtract)
         gained = keep.tile([P, PACK, S], F32)
         for t in range(PACK):
-            nc.vector.tensor_scalar(gained[:, t, :], y_plain[t], gm_sb[:, t : t + 1], None, ALU.mult)
+            nc.scalar.activation(gained[:, t, :], y_plain[t], ACT.Copy, scale=gm_sb[:, t : t + 1])
         gate = [keep.tile([P, PACK, HALF], F32, name=f"gate{h}") for h in range(2)]
         for h in range(2):
             for t in range(PACK):
                 nc.scalar.activation(gate[h][:, t, :], looked_up(st[t], n4_sb, h), ACT.Sigmoid)
         z2_bf = keep.tile([P, PACK * S], BF16, tag="held_a", align_bytes=64)
-        z2_codes = keep.tile([P, S], U32, align_bytes=64)
+        z2_codes = keep.tile([P, S], U32, tag="held_c", align_bytes=64)
         z2_scales = keep.tile([P, S], U8, align_bytes=64)
         for h in range(2):
             nc.vector.tensor_tensor(woven(z2_bf[:, cols(h, PACK * HALF)]), by_fours(gate[h][:]), by_fours(gained[:, :, cols(h)]), ALU.mult)
@@ -166,9 +169,9 @@ def tile_picked_forkclampbcubehopd_none_po_kernel(tc, x_words, x_scales, w1_word
                 nc.vector.tensor_tensor(pair[h][:, t, :], looked_up(y[t], n1_sb, h), y_plain[t][:, cols(h)], ALU.mult)
         gn_twice = keep.tile([P, PACK], F32)
         gn_minus = keep.tile([P, PACK], F32)
-        nc.vector.tensor_scalar(gn_twice[:], gn_sb[:], 2.0, 0.0, ALU.mult, ALU.add)
-        nc.vector.tensor_scalar(gn_minus[:], gn_sb[:], -1.0, 0.0, ALU.mult, ALU.add)
-        sig = [keep.tile([P, PACK, HALF], F32, name=f"sig{h}") for h in range(2)]
+        nc.gpsimd.tensor_scalar(gn_twice[:], gn_sb[:], 2.0, 0.0, ALU.mult, ALU.add)
+        nc.gpsimd.tensor_scalar(gn_minus[:], gn_sb[:], -1.0, 0.0, ALU.mult, ALU.add)
+        sig = [keep.tile([P, PACK, HALF], F32, name="sig0"), keep.tile([P, PACK, HALF], F32, name="sig1", tag="held_c", align_bytes=64)]
         bent = [keep.tile([P, PACK, HALF], F32, name=f"bent{h}") for h in range(2)]
         for h in range(2):
             for t in range(PACK):

@@ -148,9 +148,10 @@ def tile_picked_forkclampbcubehopd_none_po_kernel(tc, x_words, x_scales, w1_word
         for h in range(2):
             for t in range(PACK):
                 nc.scalar.activation(gate[h][:, t, :], looked_up(st[t], n4_sb, h), ACT.Sigmoid)
-        z2_bf = keep.tile([P, PACK * S], BF16, tag="held_a", align_bytes=64)
+        pair = keep.tile([P, PACK * S], F32, align_bytes=64)
+        z2_bf = pair[:, 2 * S :].bitcast(BF16)
         z2_codes = keep.tile([P, S], U32, tag="held_c", align_bytes=64)
-        z2_scales = keep.tile([P, S], U8, align_bytes=64)
+        z2_scales = keep.tile([P, S], U8, tag="held_d", align_bytes=64)
         for h in range(2):
             nc.vector.tensor_tensor(woven(z2_bf[:, cols(h, PACK * HALF)]), by_fours(gate[h][:]), by_fours(gained[:, :, cols(h)]), ALU.mult)
         for h in range(2):
@@ -163,64 +164,63 @@ def tile_picked_forkclampbcubehopd_none_po_kernel(tc, x_words, x_scales, w1_word
         for t in range(PACK):
             nc.scalar.copy(b[t][:, :S], b_banks[t][:])
 
-        pair = [keep.tile([P, PACK, HALF], F32, name="pair0"), keep.tile([P, PACK, HALF], F32, name="pair1", tag="held_a", align_bytes=64)]
-        for h in range(2):
-            for t in range(PACK):
-                nc.vector.tensor_tensor(pair[h][:, t, :], looked_up(y[t], n1_sb, h), y_plain[t][:, cols(h)], ALU.mult)
+        for t in range(PACK):
+            nc.vector.tensor_tensor(pair[:, cols(t, S)], y[t][:].indirect(n1_sb[:]), y_plain[t], ALU.mult)
+        pair_planes = pair[:].rearrange("p (t j) -> p t j", t=PACK)
         gn_twice = keep.tile([P, PACK], F32)
         gn_minus = keep.tile([P, PACK], F32)
         nc.gpsimd.tensor_scalar(gn_twice[:], gn_sb[:], 2.0, 0.0, ALU.mult, ALU.add)
         nc.gpsimd.tensor_scalar(gn_minus[:], gn_sb[:], -1.0, 0.0, ALU.mult, ALU.add)
         sig = [keep.tile([P, PACK, HALF], F32, name="sig0"), keep.tile([P, PACK, HALF], F32, name="sig1", tag="held_c", align_bytes=64)]
-        bent = [keep.tile([P, PACK, HALF], F32, name=f"bent{h}") for h in range(2)]
+        bent = [keep.tile([P, PACK, HALF], F32, name="bent0", tag="held_d", align_bytes=64), keep.tile([P, PACK, HALF], F32, name="bent1")]
         for h in range(2):
             for t in range(PACK):
                 nc.scalar.activation(sig[h][:, t, :], looked_up(y[t], n2_sb, h), ACT.Sigmoid, scale=2.0)
             for t in range(PACK):
                 nc.scalar.activation(bent[h][:, t, :], sig[h][:, t, :], ACT.Identity, scale=gn_twice[:, t : t + 1], bias=gn_minus[:, t : t + 1])
-        z_bf = keep.tile([P, PACK * S], BF16, tag="held_b", align_bytes=64)
+        floor = keep.tile([P, PACK * S], F32, align_bytes=64)
+        z_bf = floor[:, 2 * S :].bitcast(BF16)
         z_codes = keep.tile([P, S], U32, align_bytes=64)
         z_scales = keep.tile([P, S], U8, align_bytes=64)
-        for h in range(2):
-            nc.vector.tensor_tensor(woven(z_bf[:, cols(h, PACK * HALF)]), by_fours(pair[h][:]), by_fours(bent[h][:]), ALU.mult)
+        for engine, first, width in ((nc.gpsimd, 0, HALF), (nc.gpsimd, HALF, QUARTER), (nc.vector, HALF + QUARTER, QUARTER)):
+            h, start = divmod(first, HALF)
+            engine.tensor_tensor(
+                woven(z_bf[:, PACK * first : PACK * (first + width)]),
+                by_fours(pair_planes[:, :, first : first + width]),
+                by_fours(bent[h][:, :, start : start + width]),
+                ALU.mult,
+            )
         for h in range(2):
             nc.vector.quantize_mx(out=z_codes[:, cols(h)].bitcast(FP8X4), scales=z_scales[:, cols(h)], in_=z_bf[:, cols(h, PACK * HALF)])
         w2_codes = keep.tile([P, N], I32, align_bytes=64)
         deal_columns(w2_codes[:], w2_raw[:])
         a_banks = product("ab", w2_codes, w23_dealt[:], z_codes, z_scales)
-        a_half = planes_tile("a_half")
         a_plain = planes_tile("a_plain")
         for t in range(PACK):
-            nc.scalar.activation(a_half[t][:], a_banks[t][:], ACT.Copy, scale=-0.5)
+            nc.scalar.activation(y[t][:, :S], a_banks[t][:], ACT.Copy, scale=-0.5)
             nc.scalar.copy(a_plain[t][:], a_banks[t][:])
 
         ceiling = keep.tile([P, PACK, S], F32)
         for t in range(PACK):
             nc.vector.tensor_copy(ceiling[:, t, :], b[t][:].indirect(n6_sb[:]))
-        floor = [keep.tile([P, PACK, HALF], F32, name="floor0"), keep.tile([P, PACK, HALF], F32, name="floor1", tag="held_b", align_bytes=64)]
-        for h in range(2):
-            for t in range(PACK):
-                nc.vector.tensor_copy(floor[h][:, t, :], looked_up(b[t], n7_sb, h))
+        for t in range(PACK):
+            nc.vector.tensor_copy(floor[:, cols(t, S)], b[t][:].indirect(n7_sb[:]))
+        floor_planes = floor[:].rearrange("p (t j) -> p t j", t=PACK)
 
         out_codes = keep.tile([P, S], U32, align_bytes=64)
         out_scales = keep.tile([P, S], U8, align_bytes=64)
         out_rows = out_0.rearrange("(p t) j -> p t j", t=PACK)
         out_words = words_in_hbm(out_1)
-        pieces = [(0, 0, HALF), (1, 0, QUARTER), (1, QUARTER, QUARTER)]
-        less = [keep.tile([P, PACK, HALF], F32, name=f"less{h}") for h in range(2)]
-        for h in range(2):
+        less = keep.tile([P, PACK, S], F32)
+        capped = keep.tile([P, PACK, S], F32)
+        for h, pieces in enumerate((((0, HALF),), ((HALF, QUARTER), (HALF + QUARTER, QUARTER)))):
             for t in range(PACK):
-                nc.vector.tensor_tensor(less[h][:, t, :], looked_up(a_half[t], n5_sb, h), a_plain[t][:, cols(h)], ALU.add)
-            for h2, start, width in pieces:
-                if h2 != h:
-                    continue
-                inside = slice(start, start + width)
-                first = h * HALF + start
+                nc.vector.tensor_tensor(less[:, t, cols(h)], looked_up(y[t], n5_sb, h), a_plain[t][:, cols(h)], ALU.add)
+            nc.vector.tensor_tensor(capped[:, :, cols(h)], less[:, :, cols(h)], ceiling[:, :, cols(h)], ALU.min)
+            for first, width in pieces:
                 columns = slice(first, first + width)
-                capped = keep.tile([P, PACK, width], F32, name=f"capped{first}")
-                nc.vector.tensor_tensor(capped[:], less[h][:, :, inside], ceiling[:, :, columns], ALU.min)
                 result = keep.tile([P, PACK, width], F32, name=f"result{first}")
-                nc.vector.tensor_tensor(result[:], capped[:], floor[h][:, :, inside], ALU.max)
+                nc.vector.tensor_tensor(result[:], capped[:, :, columns], floor_planes[:, :, columns], ALU.max)
                 nc.sync.dma_start(out=out_rows[:, :, columns], in_=result[:])
                 result_bf = keep.tile([P, PACK * width], BF16, name=f"result_bf{first}", align_bytes=64)
                 if first + width < S:

@@ -20,7 +20,7 @@ PACK = 4
 HALF = S // 2
 QUARTER = S // 4
 LANES = 16
-COPIES_ON_VECTOR = 2
+COPIES_ON_VECTOR = 3
 
 
 def tile_picked_forkclampbcubehopd_none_po_kernel(tc, x_words, x_scales, w1_words, w1_scales, gn, w2_words, w2_scales, gm, w3_words, w3_scales, offs, n1, n2, n3, n4, n5, n6, n7, out_0, out_1, out_2):
@@ -143,7 +143,7 @@ def tile_picked_forkclampbcubehopd_none_po_kernel(tc, x_words, x_scales, w1_word
             nc.vector.tensor_tensor(st[t][:], y[t][:].indirect(n3_sb[:]), y_plain[t], ALU.subtract)
         gained = keep.tile([P, PACK, S], F32)
         for t in range(PACK):
-            nc.scalar.activation(gained[:, t, :], y_plain[t], ACT.Copy, scale=gm_sb[:, t : t + 1])
+            nc.scalar.activation(gained[:, t, :], y[t][:, :S], ACT.Copy, scale=gm_sb[:, t : t + 1])
         gate = [keep.tile([P, PACK, HALF], F32, name=f"gate{h}") for h in range(2)]
         for h in range(2):
             for t in range(PACK):
@@ -216,9 +216,9 @@ def tile_picked_forkclampbcubehopd_none_po_kernel(tc, x_words, x_scales, w1_word
         for h, pieces in enumerate((((0, HALF),), ((HALF, QUARTER), (HALF + QUARTER, QUARTER)))):
             for t in range(PACK):
                 nc.vector.tensor_tensor(less[:, t, cols(h)], looked_up(y[t], n5_sb, h), a_plain[t][:, cols(h)], ALU.add)
-            nc.vector.tensor_tensor(capped[:, :, cols(h)], less[:, :, cols(h)], ceiling[:, :, cols(h)], ALU.min)
             for first, width in pieces:
                 columns = slice(first, first + width)
+                nc.vector.tensor_tensor(capped[:, :, columns], less[:, :, columns], ceiling[:, :, columns], ALU.min)
                 result = keep.tile([P, PACK, width], F32, name=f"result{first}")
                 nc.vector.tensor_tensor(result[:], capped[:, :, columns], floor_planes[:, :, columns], ALU.max)
                 nc.sync.dma_start(out=out_rows[:, :, columns], in_=result[:])

@@ -182,7 +182,7 @@ def tile_picked_forkclampbcubehopd_none_po_kernel(tc, x_words, x_scales, w1_word
         z_bf = floor[:, 2 * S :].bitcast(BF16)
         z_codes = keep.tile([P, S], U32, align_bytes=64)
         z_scales = keep.tile([P, S], U8, align_bytes=64)
-        for engine, first, width in ((nc.gpsimd, 0, HALF), (nc.gpsimd, HALF, QUARTER), (nc.vector, HALF + QUARTER, QUARTER)):
+        for engine, first, width in ((nc.gpsimd, 0, HALF), (nc.gpsimd, HALF, HALF)):
             h, start = divmod(first, HALF)
             engine.tensor_tensor(
                 woven(z_bf[:, PACK * first : PACK * (first + width)]),

from contextlib import ExitStack

import concourse.mybir as mybir

K, T, S, N, H = 512, 2048, 512, 512, 512
FLOPS = 2 * K * H * S + 2 * 2 * H * N * S

F32 = mybir.dt.float32
BF16 = mybir.dt.bfloat16
I32 = mybir.dt.int32
U32 = mybir.dt.uint32
U16 = mybir.dt.uint16
U8 = mybir.dt.uint8
FP8X4 = mybir.dt.float8_e4m3fn_x4
ALU = mybir.AluOpType
ACT = mybir.ActivationFunctionType

P = 128
PACK = 4
HALF = S // 2
QUARTER = S // 4
LANES = 16
COPIES_ON_VECTOR = 3


def tile_picked_forkclampbcubehopd_none_po_kernel(tc, x_words, x_scales, w1_words, w1_scales, gn, w2_words, w2_scales, gm, w3_words, w3_scales, offs, n1, n2, n3, n4, n5, n6, n7, out_0, out_1, out_2):
    nc = tc.nc

    def words_in_hbm(words):
        return words[0].rearrange("p c r -> p (c r)").bitcast(I32)

    def load_scale_rows(queue, plane, first_row, scales):
        for q in range(4):
            row = 32 * q + first_row
            queue.dma_start(out=plane[row : row + 4, :].bitcast(I32), in_=scales[0, 4 * q : 4 * q + 4, :].bitcast(I32))

    def deal_columns(dealt, raw):
        nc.vector.tensor_copy(
            out=dealt.rearrange("p (t c i) -> p c t i", t=PACK, i=4),
            in_=raw.rearrange("p (c i t) -> p c t i", t=PACK, i=4),
        )

    def cols(h, width=HALF):
        return slice(h * width, (h + 1) * width)

    def looked_up(window, places, h, width=HALF):
        return window[:].indirect(places[:, h * width // LANES : (h + 1) * width // LANES])

    def by_fours(planes):
        return planes.rearrange("p t (c i) -> p c t i", i=4)

    def woven(tile):
        return tile.rearrange("p (c i t) -> p c t i", i=4, t=PACK)

    with ExitStack() as ctx:
        keep = ctx.enter_context(tc.tile_pool(name="keep", bufs=1))
        psum = ctx.enter_context(tc.psum_pool(name="psum", bufs=1))

        def load_list(name, places):
            tile = keep.tile([P, S // LANES], U16, name=name)
            nc.sync.dma_start(tile[:], places)
            return tile

        def planes_tile(name):
            return [keep.tile([P, S], F32, name=f"{name}{t}") for t in range(PACK)]

        x_plane = keep.tile([P, T], U8)
        nc.gpsimd.memset(x_plane[:].bitcast(I32), 0)
        w1_plane = keep.tile([P, H], U8)
        nc.vector.memset(w1_plane[:].bitcast(I32), 0)
        w23_plane = keep.tile([P, N], U8)
        nc.vector.memset(w23_plane[:].bitcast(I32), 0)
        warm = keep.tile([P, 2], F32)
        nc.vector.memset(warm[:, 0:1], 0.0)
        nc.scalar.activation(warm[:, 1:2], warm[:, 0:1], ACT.Sigmoid)

        y = [keep.tile([P, 2 * S], F32, name=f"y{t}") for t in range(PACK)]
        for t in range(PACK):
            nc.vector.memset(y[t][:, S:], 0.0)

        offs_sb = load_list("offs_sb", offs)
        load_scale_rows(nc.sync, x_plane, 0, x_scales)
        w1_raw = keep.tile([P, H], I32)
        nc.sync.dma_start(out=w1_raw[:], in_=words_in_hbm(w1_words))
        x_codes = keep.tile([P, T], I32)
        nc.sync.dma_start(out=x_codes[:], in_=words_in_hbm(x_words))
        n3_sb = load_list("n3_sb", n3)
        load_scale_rows(nc.sync, w1_plane, 0, w1_scales)
        w3_raw = keep.tile([P, N], I32)
        nc.sync.dma_start(out=w3_raw[:], in_=words_in_hbm(w3_words))
        w2_raw = keep.tile([P, N], I32)
        nc.sync.dma_start(out=w2_raw[:], in_=words_in_hbm(w2_words))
        load_scale_rows(nc.sync, w23_plane, 4, w3_scales)
        load_scale_rows(nc.sync, w23_plane, 0, w2_scales)
        gm_sb = keep.tile([P, PACK], F32)
        nc.sync.dma_start(out=gm_sb[:], in_=gm.rearrange("(p t) o -> p (t o)", t=PACK))
        n4_sb = load_list("n4_sb", n4)
        n1_sb = load_list("n1_sb", n1)
        n2_sb = load_list("n2_sb", n2)
        gn_sb = keep.tile([P, PACK], F32)
        nc.sync.dma_start(out=gn_sb[:], in_=gn.rearrange("(p t) o -> p (t o)", t=PACK))
        n6_sb = load_list("n6_sb", n6)
        n7_sb = load_list("n7_sb", n7)
        n5_sb = load_list("n5_sb", n5)

        w1_codes = keep.tile([P, H], I32, align_bytes=64)
        deal_columns(w1_codes[:], w1_raw[:])
        xq_scales = keep.tile([P, S], U8, align_bytes=64)
        nc.vector.tensor_copy(xq_scales[:], x_plane[:].indirect(offs_sb[:]))
        xq_codes = keep.tile([P, S], U32, align_bytes=64)
        nc.vector.tensor_copy(xq_codes[:, cols(0)], x_codes[:].bitcast(U32).indirect(offs_sb[:, : HALF // LANES]))
        w1_dealt = keep.tile([P, H], U8, align_bytes=64)
        deal_columns(w1_dealt[:], w1_plane[:])
        nc.vector.tensor_copy(xq_codes[:, cols(1)], x_codes[:].bitcast(U32).indirect(offs_sb[:, HALF // LANES :]))

        def product(name, w_codes, w_scales, codes, scales):
            banks = [psum.tile([P, S], F32, name=f"{name}{t}") for t in range(PACK)]
            for t in range(PACK):
                for h in range(2):
                    nc.tensor.matmul_mx(
                        out=banks[t][:, cols(h)],
                        lhsT=w_codes[:, cols(t, P)].bitcast(FP8X4),
                        lhsT_scale=w_scales[:, cols(t, P)],
                        rhs=codes[:, cols(h)].bitcast(FP8X4),
                        rhs_scale=scales[:, cols(h)],
                        start=True,
                        stop=True,
                    )
            return banks

        y_banks = product("ab", w1_codes, w1_dealt[:], xq_codes, xq_scales)
        b = [keep.tile([P, 2 * S], F32, name=f"b_sb{t}") for t in range(PACK)]
        y_plain = [b[t][:, S:] for t in range(PACK)]
        for t in range(PACK):
            nc.scalar.copy(y[t][:, :S], y_banks[t][:])
            if t < COPIES_ON_VECTOR:
                nc.vector.tensor_copy(y_plain[t], y[t][:, :S])
            else:
                nc.scalar.copy(y_plain[t], y_banks[t][:])

        st = planes_tile("st")
        for t in range(PACK):
            nc.vector.tensor_tensor(st[t][:], y[t][:].indirect(n3_sb[:]), y_plain[t], ALU.subtract)
        gained = keep.tile([P, PACK, S], F32)
        for t in range(PACK):
            nc.scalar.activation(gained[:, t, :], y[t][:, :S], ACT.Copy, scale=gm_sb[:, t : t + 1])
        gate = [keep.tile([P, PACK, HALF], F32, name=f"gate{h}") for h in range(2)]
        for h in range(2):
            for t in range(PACK):
                nc.scalar.activation(gate[h][:, t, :], looked_up(st[t], n4_sb, h), ACT.Sigmoid)
        pair = keep.tile([P, PACK * S], F32, align_bytes=64)
        z2_bf = pair[:, 2 * S :].bitcast(BF16)
        z2_codes = keep.tile([P, S], U32, tag="held_c", align_bytes=64)
        z2_scales = keep.tile([P, S], U8, tag="held_d", align_bytes=64)
        for h in range(2):
            nc.vector.tensor_tensor(woven(z2_bf[:, cols(h, PACK * HALF)]), by_fours(gate[h][:]), by_fours(gained[:, :, cols(h)]), ALU.mult)
        for h in range(2):
            nc.vector.quantize_mx(out=z2_codes[:, cols(h)].bitcast(FP8X4), scales=z2_scales[:, cols(h)], in_=z2_bf[:, cols(h, PACK * HALF)])
        w3_codes = keep.tile([P, N], I32, align_bytes=64)
        deal_columns(w3_codes[:], w3_raw[:])
        w23_dealt = keep.tile([P, N], U8, align_bytes=64)
        deal_columns(w23_dealt[:], w23_plane[:])
        b_banks = product("b", w3_codes, w23_dealt[4:, :], z2_codes, z2_scales)
        for t in range(PACK):
            nc.scalar.copy(b[t][:, :S], b_banks[t][:])

        for t in range(PACK):
            nc.vector.tensor_tensor(pair[:, cols(t, S)], y[t][:].indirect(n1_sb[:]), y_plain[t], ALU.mult)
        pair_planes = pair[:].rearrange("p (t j) -> p t j", t=PACK)
        gn_twice = keep.tile([P, PACK], F32)
        gn_minus = keep.tile([P, PACK], F32)
        nc.gpsimd.tensor_scalar(gn_twice[:], gn_sb[:], 2.0, 0.0, ALU.mult, ALU.add)
        nc.gpsimd.tensor_scalar(gn_minus[:], gn_sb[:], -1.0, 0.0, ALU.mult, ALU.add)
        sig = [keep.tile([P, PACK, HALF], F32, name="sig0"), keep.tile([P, PACK, HALF], F32, name="sig1", tag="held_c", align_bytes=64)]
        bent = [keep.tile([P, PACK, HALF], F32, name="bent0", tag="held_d", align_bytes=64), keep.tile([P, PACK, HALF], F32, name="bent1")]
        for h in range(2):
            for t in range(PACK):
                nc.scalar.activation(sig[h][:, t, :], looked_up(y[t], n2_sb, h), ACT.Sigmoid, scale=2.0)
            for t in range(PACK):
                nc.scalar.activation(bent[h][:, t, :], sig[h][:, t, :], ACT.Identity, scale=gn_twice[:, t : t + 1], bias=gn_minus[:, t : t + 1])
        floor = keep.tile([P, PACK * S], F32, align_bytes=64)
        z_bf = floor[:, 2 * S :].bitcast(BF16)
        z_codes = keep.tile([P, S], U32, align_bytes=64)
        z_scales = keep.tile([P, S], U8, align_bytes=64)
        for engine, first, width in ((nc.gpsimd, 0, HALF), (nc.gpsimd, HALF, HALF)):
            h, start = divmod(first, HALF)
            engine.tensor_tensor(
                woven(z_bf[:, PACK * first : PACK * (first + width)]),
                by_fours(pair_planes[:, :, first : first + width]),
                by_fours(bent[h][:, :, start : start + width]),
                ALU.mult,
            )
        for h in range(2):
            nc.vector.quantize_mx(out=z_codes[:, cols(h)].bitcast(FP8X4), scales=z_scales[:, cols(h)], in_=z_bf[:, cols(h, PACK * HALF)])
        w2_codes = keep.tile([P, N], I32, align_bytes=64)
        deal_columns(w2_codes[:], w2_raw[:])
        a_banks = product("ab", w2_codes, w23_dealt[:], z_codes, z_scales)
        a_plain = planes_tile("a_plain")
        for t in range(PACK):
            nc.scalar.activation(y[t][:, :S], a_banks[t][:], ACT.Copy, scale=-0.5)
            nc.scalar.copy(a_plain[t][:], a_banks[t][:])

        ceiling = keep.tile([P, PACK, S], F32)
        for t in range(PACK):
            nc.vector.tensor_copy(ceiling[:, t, :], b[t][:].indirect(n6_sb[:]))
        for t in range(PACK):
            nc.vector.tensor_copy(floor[:, cols(t, S)], b[t][:].indirect(n7_sb[:]))
        floor_planes = floor[:].rearrange("p (t j) -> p t j", t=PACK)

        out_codes = keep.tile([P, S], U32, align_bytes=64)
        out_scales = keep.tile([P, S], U8, align_bytes=64)
        out_rows = out_0.rearrange("(p t) j -> p t j", t=PACK)
        out_words = words_in_hbm(out_1)
        less = keep.tile([P, PACK, S], F32)
        capped = keep.tile([P, PACK, S], F32)
        for h, pieces in enumerate((((0, HALF),), ((HALF, QUARTER), (HALF + QUARTER, QUARTER)))):
            for t in range(PACK):
                nc.vector.tensor_tensor(less[:, t, cols(h)], looked_up(y[t], n5_sb, h), a_plain[t][:, cols(h)], ALU.add)
            for first, width in pieces:
                columns = slice(first, first + width)
                nc.vector.tensor_tensor(capped[:, :, columns], less[:, :, columns], ceiling[:, :, columns], ALU.min)
                result = keep.tile([P, PACK, width], F32, name=f"result{first}")
                nc.vector.tensor_tensor(result[:], capped[:, :, columns], floor_planes[:, :, columns], ALU.max)
                nc.sync.dma_start(out=out_rows[:, :, columns], in_=result[:])
                result_bf = keep.tile([P, PACK * width], BF16, name=f"result_bf{first}", align_bytes=64)
                if first + width < S:
                    nc.scalar.copy(woven(result_bf[:]), by_fours(result[:]))
                else:
                    nc.vector.tensor_copy(woven(result_bf[:]), by_fours(result[:]))
                nc.vector.quantize_mx(out=out_codes[:, columns].bitcast(FP8X4), scales=out_scales[:, columns], in_=result_bf[:])
            nc.sync.dma_start(out=out_words[:, cols(h)], in_=out_codes[:, cols(h)].bitcast(I32))
        for q in range(4):
            queue = nc.scalar if q % 2 else nc.sync
            queue.dma_start(out=out_2[0, 4 * q : 4 * q + 4, :].bitcast(I32), in_=out_scales[32 * q : 32 * q + 4, :].bitcast(I32))
